import numpy as np
import ml_dtypes


def mxq(x, axis, fmt="e4m3"):
    dtype, down = {"e4m3": (ml_dtypes.float8_e4m3fn, 7), "e5m2": (ml_dtypes.float8_e5m2, 14)}[fmt]
    v = np.moveaxis(np.asarray(x, np.float32).astype(ml_dtypes.bfloat16).astype(np.float64), axis, -1)
    blocks = v.reshape(v.shape[:-1] + (-1, 32))
    amax = np.abs(blocks).max(-1, keepdims=True)
    byte = np.maximum(np.where(amax > 0, np.frexp(amax)[1] - 1 + 127, 0) - down, 1)
    scale = np.exp2(byte - 127.0)
    codes = (blocks / scale).astype(np.float32).astype(dtype).astype(np.float64)
    return np.moveaxis((codes * scale).reshape(v.shape), -1, axis)


WIDE = False


def mx_kscale(k):
    if not WIDE:
        return np.ones(k)
    levels = np.array([10, -10, 5, -5, 0])
    if k % 512:
        return np.exp2(np.random.permutation(np.resize(levels, k // 32))).repeat(32)
    a = np.empty((k // 512, 16))
    for p in range(k // 512):
        a[p, :8] = np.random.permutation(np.resize(levels, 8))
        for g in range(8):
            far = levels[np.abs(levels - a[p, g]) >= 10]
            a[p, g + 8] = far[np.random.randint(len(far))]
    return np.exp2(a.ravel()).repeat(32)


BF16 = ml_dtypes.bfloat16


def bf(x):
    return np.asarray(x, np.float32).astype(BF16)


def f64(x):
    return np.asarray(x).astype(np.float64)

def planes(Y):
    n, m = Y.shape
    b = f64(bf(Y)).reshape(n // 32, 32, m)
    amax = np.abs(b).max(1)
    byte = np.clip(np.where(amax > 0, np.frexp(amax)[1] - 1 + 127 - 7, 1), 1, 254)
    codes = (b * np.exp2(127.0 - byte)[:, None, :]).reshape(n, m).astype(np.float32).astype(ml_dtypes.float8_e4m3fn).view(np.uint8)
    words = codes.reshape(n // 512, 128, 4, m).transpose(0, 1, 3, 2)
    return np.ascontiguousarray(words), np.ascontiguousarray(byte.astype(np.uint8).reshape(n // 512, 16, m))


H, S, T, G, D, DV = 2, 1024, 1024, 128, 512, 512
W = T // G


def softmax_last(x):
    e = np.exp(x - np.max(x, axis=-1, keepdims=True))
    return e / np.sum(e, axis=-1, keepdims=True)


def setup_inputs():
    s, t = mx_kscale(D), mx_kscale(T)
    return {
        "q": bf(np.random.standard_normal((H, S, D)) * s),
        "k": bf(np.random.standard_normal((H, T, D)) / s),
        "lm": bf(np.random.standard_normal((H, G, D)) * 1.5 / s),
        "gain": bf(np.random.standard_normal((H, T)) * 4.0 * t),
        "v": bf(np.random.standard_normal((H, T, DV)) / t[:, None]),
    }


def core(q, k, lm, gain, v):
    root = np.sqrt(D)
    qq = mxq(f64(q), 2, "e4m3")
    s = (qq @ mxq(f64(k), 2, "e4m3").transpose(0, 2, 1)) / root
    r = (qq @ mxq(f64(lm), 2, "e4m3").transpose(0, 2, 1)) / root
    pin = softmax_last(s.reshape(H, S, G, W))
    pg = softmax_last(r)
    p = (pg[:, :, :, None] * pin).reshape(H, S, T)
    pt = p * f64(gain)[:, None, :]
    return mxq(pt, 2, "e4m3") @ mxq(f64(v), 1, "e4m3")


def reference(q, k, lm, gain, v):
    R_out = core(q, k, lm, gain, v)
    words, scales = planes(np.moveaxis(R_out, 1, 0).reshape(1024, -1))
    return R_out, words, scales

from contextlib import ExitStack

import concourse.mybir as mybir
from concourse.masks import make_identity

H, S, T, G, D, DV = 2, 1024, 1024, 128, 512, 512
FLOPS = 2 * H * S * D * (T + G) + 2 * H * S * T * DV

F32 = mybir.dt.float32
BF16 = mybir.dt.bfloat16
U32 = mybir.dt.uint32
I32 = mybir.dt.int32
U8 = mybir.dt.uint8
FP8X4 = mybir.dt.float8_e4m3fn_x4
ALU = mybir.AluOpType
ACT = mybir.ActivationFunctionType
AX = mybir.AxisListType

INV = 1.0 / 512.0**0.5
P = 128


def tile_landmarkgroupedsoftmaxattention_x1_kernel(tc, q, k, lm, gain, v, out_0, out_1, out_2):
    nc = tc.nc
    with ExitStack() as ctx:
        const = ctx.enter_context(tc.tile_pool(name="const", bufs=1))
        raws = ctx.enter_context(tc.tile_pool(name="raws", bufs=5))
        stage = ctx.enter_context(tc.tile_pool(name="stage", bufs=3))
        keep = ctx.enter_context(tc.tile_pool(name="keep", bufs=1))
        small = ctx.enter_context(tc.tile_pool(name="small", bufs=4))
        probs = ctx.enter_context(tc.tile_pool(name="probs", bufs=2))
        outs = ctx.enter_context(tc.tile_pool(name="outs", bufs=2))
        psum = ctx.enter_context(tc.psum_pool(name="psum", bufs=4))
        ctx.enter_context(tc.manual_schedule())

        ident = const.tile([P, P], F32, name="ident")
        make_identity(nc, ident[:])
        gain_b = const.tile([P, 4, 4], BF16, name="gain_b")
        gain_f = const.tile([P, 4, 4], F32, name="gain_f")

        def load(x, h, c, parts=1):
            raw = raws.tile([P, 4, 512], BF16, name="raw", tag="raw", bufs=5, align_bytes=64)
            src = x[h, 512 * c : 512 * c + 512, :].rearrange("(p t) d -> p t d", t=4)
            w = 4 // parts
            for a in range(parts):
                nc.sync.dma_start(out=raw[:, w * a : w * a + w, :], in_=src[:, w * a : w * a + w, :])
            return raw

        def load_lm(h):
            raw = raws.tile([P, 512], BF16, name="raw_lm", tag="raw_lm", bufs=2, align_bytes=64)
            nc.sync.dma_start(out=raw[:], in_=lm[h, :, :])
            return raw

        def copy_on(engine, out, in_):
            if engine == "s":
                nc.scalar.copy(out, in_)
            else:
                nc.vector.tensor_copy(out=out, in_=in_)

        def turn_piece(raw, grouped, j, engine):
            words = raw[:].rearrange("p t d -> p (t d)").bitcast(F32)
            tp = psum.tile([P, 2, 2, P], F32, name="tp", tag="o", bufs=4)
            for a in range(2):
                for u in range(2):
                    base = 256 * (2 * j + a)
                    nc.tensor.transpose(tp[:, a, u, :], words[:, base + u : base + 256 : 2], ident[:])
            dst = grouped[:, 256 * j : 256 * j + 256, :].rearrange("p r t -> p (r t)").bitcast(F32)
            copy_on(engine, dst.rearrange("p (a r u) -> p a r u", a=2, u=2), tp[:].rearrange("p a u r -> p a r u"))

        def turn_lm(raw, grouped, engine):
            words = raw[:].bitcast(F32)
            tp = psum.tile([P, 2, P], F32, name="tpl", tag="o", bufs=4)
            for u in range(2):
                nc.tensor.transpose(tp[:, u, :], words[:, u:256:2], ident[:])
            dst = grouped[:].rearrange("p r t -> p (r t)").bitcast(F32)
            copy_on(engine, dst.rearrange("p (r u) -> p r u", u=2), tp[:].rearrange("p u r -> p r u"))

        def new_grouped():
            return stage.tile([P, 512, 4], BF16, name="grouped", tag="grouped", bufs=4, align_bytes=64)

        def quantize(grouped, name, n=512):
            codes = keep.tile([P, n], U32, name=name + "_c", tag=name + "_c", bufs=1, align_bytes=64)
            scales = keep.tile([P, n], U8, name=name + "_s", tag=name + "_s", bufs=1, align_bytes=64)
            nc.vector.quantize_mx(
                out=codes[:].bitcast(FP8X4), scales=scales[:], in_=grouped[:].rearrange("p n t -> p (n t)")
            )
            return codes, scales

        def mx(out, lhs, lcols, rhs, rcols, start=True, stop=True):
            nc.tensor.matmul_mx(
                out=out,
                lhsT=lhs[0][:, lcols].bitcast(FP8X4),
                lhsT_scale=lhs[1][:, lcols],
                rhs=rhs[0][:, rcols].bitcast(FP8X4),
                rhs_scale=rhs[1][:, rcols],
                start=start,
                stop=stop,
            )

        ALL = slice(0, 512)

        def blk(i):
            return slice(P * i, P * i + P)

        kq, qq, lq, vq = {}, {}, {}, {}
        raw = {}
        raw["k", 0, 0] = load(k, 0, 0, 2)
        raw["q", 0, 0] = load(q, 0, 0, 2)
        raw["k", 0, 1] = load(k, 0, 1)
        raw["lm", 0] = load_lm(0)
        raw["q", 0, 1] = load(q, 0, 1)
        nc.sync.dma_start(out=gain_b[:], in_=gain.rearrange("h (c p t) -> p (h c) t", c=2, t=4))

        def new_lm_grouped():
            return stage.tile([P, P, 4], BF16, name="lgrouped", tag="lgrouped", bufs=2, align_bytes=64)

        grp = {}
        e, st, mt, zt = {}, {}, {}, {}
        L0, R, nR, Z, lnZ, rt = {}, {}, {}, {}, {}, {}
        lnzT, lnz, y1, ydup, cg = {}, {}, {}, {}, {}
        for h in range(H):
            for d, nm in ((R, "R"), (nR, "nR"), (Z, "Z"), (lnZ, "lnZ")):
                d[h] = const.tile([P, 8], F32, name="%s%d" % (nm, h))

        def piece(key, j, engine="s"):
            if key[0] == "lm":
                grp[key] = new_lm_grouped()
                turn_lm(raw[key], grp[key], engine)
            else:
                if j == 0:
                    grp[key] = new_grouped()
                turn_piece(raw[key], grp[key], j, engine)

        def quant(key):
            nm = key[0] + "".join(str(x) for x in key[1:])
            dst = {"k": kq, "q": qq, "v": vq, "lm": lq}[key[0]]
            dst[key[1:]] = quantize(grp[key], nm, P if key[0] == "lm" else 512)

        def v_group(h, c):
            g = stage.tile([P, 512, 4], BF16, name="vgrouped", tag="grouped", bufs=4, align_bytes=64)
            nc.gpsimd.tensor_scalar(
                out=g[:], in0=raw["v", h, c][:].rearrange("p t n -> p n t"), scalar1=1.0, scalar2=0.0, op0=ALU.mult, op1=ALU.add
            )
            grp["v", h, c] = g

        def mm_s(i, c):
            st[i, c] = psum.tile([P, 512], F32, name="s", tag="s", bufs=4)
            mx(st[i, c][:], qq[i // 8, (i % 8) // 4], blk(i % 4), kq[i // 8, c], ALL)

        def vmax(i, c):
            mt[i, c] = small.tile([P, 64], F32, name="m", tag="m", bufs=4)
            nc.vector.tensor_reduce(
                out=mt[i, c][:], in_=st[i, c][:].rearrange("p (t g h) -> p g t h", t=4, h=2), axis=AX.XY, op=ALU.max
            )

        def vsub(i, c):
            if i not in e:
                e[i] = keep.tile([P, 4, 2, P], F32, name="e%d" % i, tag="e%d" % i, bufs=1)
            nc.vector.tensor_tensor(
                out=e[i][:, :, c, :].rearrange("p t (g h) -> p t g h", h=2),
                in0=st[i, c][:].rearrange("p (t g h) -> p t g h", t=4, h=2),
                in1=mt[i, c][:].unsqueeze(1).unsqueeze(3).to_broadcast([P, 4, 64, 2]),
                op=ALU.subtract,
            )

        def s_exp(i):
            flat = e[i][:].rearrange("p t c n -> p (t c n)")
            nc.scalar.activation(out=flat, in_=flat, func=ACT.Exp, scale=INV)

        def pe_z(i):
            h, u = i // 8, (i % 8) // 4
            if i % 4 == 0:
                zt[h, u] = psum.tile([P, 4, P], F32, name="zt", tag="o", bufs=4)
            flat = e[i][:].rearrange("p t c n -> p (t c n)")
            for x in range(8):
                t, half = x // 2, x % 2
                nc.tensor.matmul(
                    zt[h, u][:, i % 4, :],
                    lhsT=flat[:, 256 * t + half : 256 * t + 256 : 2],
                    rhs=ident[:],
                    start=(x == 0),
                    stop=(x == 7),
                    is_transpose=True,
                )

        def pe_r(h, u):
            rt[h, u] = psum.tile([P, 4, P], F32, name="r", tag="o", bufs=4)
            for i in range(4):
                mx(rt[h, u][:, i, :], qq[h, u], blk(i), lq[(h,)], blk(0))

        def v_R(h, u):
            nc.vector.tensor_reduce(out=R[h][:, 4 * u : 4 * u + 4], in_=rt[h, u][:], axis=AX.X, op=ALU.max)

        def v_nR(h, u):
            nc.vector.tensor_scalar(
                out=nR[h][:, 4 * u : 4 * u + 4], in0=R[h][:, 4 * u : 4 * u + 4], scalar1=-INV, scalar2=None, op0=ALU.mult
            )

        def s_L(h, u):
            L0[h, u] = small.tile([P, 4, P], F32, name="L0", tag="L0", bufs=3)
            for i in range(4):
                nc.scalar.activation(
                    out=L0[h, u][:, i, :], in_=rt[h, u][:, i, :], func=ACT.Identity, scale=INV, bias=nR[h][:, 4 * u + i : 4 * u + i + 1]
                )

        def s_Z(h, u):
            for i in range(4):
                junk = small.tile([P, P], F32, name="junk", tag="junk", bufs=2)
                nc.scalar.activation(
                    out=junk[:], in_=L0[h, u][:, i, :], func=ACT.Exp, accum_out=Z[h][:, 4 * u + i : 4 * u + i + 1]
                )

        def s_ln(h):
            for u in range(2):
                lnzT[h, u] = small.tile([P, 4, P], F32, name="lnzT", tag="lnzT", bufs=2)
                nc.scalar.activation(out=lnzT[h, u][:], in_=zt[h, u][:], func=ACT.Ln)
            nc.scalar.activation(out=lnZ[h][:], in_=Z[h][:], func=ACT.Ln)

        def pe_lnz(h, u):
            lnz[h, u] = psum.tile([P, 4, P], F32, name="lnz", tag="o", bufs=4)
            for i in range(4):
                nc.tensor.transpose(lnz[h, u][:, i, :], lnzT[h, u][:, i, :], ident[:])

        def v_y(h, u):
            y1[h, u] = small.tile([P, 4, P], F32, name="y1", tag="y1", bufs=2)
            for i in range(4):
                nc.vector.scalar_tensor_tensor(
                    out=y1[h, u][:, i, :],
                    in0=L0[h, u][:, i, :],
                    scalar=lnZ[h][:, 4 * u + i : 4 * u + i + 1],
                    in1=lnz[h, u][:, i, :],
                    op0=ALU.subtract,
                    op1=ALU.subtract,
                )
            ydup[h, u] = small.tile([P, 4 * P, 2], F32, name="ydup", tag="ydup", bufs=2)
            nc.gpsimd.tensor_scalar(
                out=ydup[h, u][:],
                in0=y1[h, u][:].rearrange("p i g -> p (i g)").unsqueeze(2).to_broadcast([P, 4 * P, 2]),
                scalar1=1.0,
                scalar2=0.0,
                op0=ALU.mult,
                op1=ALU.add,
            )

        def make_cg(h, u, c):
            yT = psum.tile([P, 4, P], F32, name="yT", tag="o", bufs=4)
            flat = ydup[h, u][:].rearrange("p g h -> p (g h)")
            for i in range(4):
                nc.tensor.transpose(yT[:, i, :], flat[:, 256 * i + P * c : 256 * i + P * c + P], ident[:])
            cT = small.tile([P, 512], F32, name="cT", tag="cT", bufs=2)
            nc.scalar.activation(out=cT[:], in_=yT[:].rearrange("p i n -> p (i n)"), func=ACT.Exp)
            cg[h, u, c] = probs.tile([P, 4, 512], F32, name="cg", tag="cg", bufs=3)
            for t in range(4):
                nc.gpsimd.tensor_scalar(
                    out=cg[h, u, c][:, t, :],
                    in0=cT[:],
                    scalar1=gain_f[:, 2 * h + c, t : t + 1],
                    scalar2=0.0,
                    op0=ALU.mult,
                    op1=ALU.add,
                )

        eT, pt, ptq, o, ob = {}, {}, {}, {}, {}
        steps = []
        for h in range(H):
            for u in range(2):
                if (h, u) == (1, 1):
                    steps += [(h, u, c, i) for i in range(4) for c in range(2)]
                else:
                    steps += [(h, u, c, i) for c in range(2) for i in range(4)]

        def pe_eT(n):
            h, u, c, i = steps[n]
            eT[n] = psum.tile([P, 4, P], F32, name="eT", tag="s", bufs=4)
            for t in range(4):
                nc.tensor.transpose(eT[n][:, t, :], e[8 * h + 4 * u + i][:, t, c, :], ident[:])

        def v_tt(n):
            h, u, c, i = steps[n]
            if i == 0:
                pt[h, u, c] = probs.tile([P, 512, 4], BF16, name="pt", tag="pt", bufs=2, align_bytes=64)
                ptq[h, u, c] = (
                    probs.tile([P, 512], U32, name="ptc", tag="ptc", bufs=4, align_bytes=64),
                    probs.tile([P, 512], U8, name="pts", tag="pts", bufs=4, align_bytes=64),
                )
            nc.vector.tensor_tensor(
                out=pt[h, u, c][:, blk(i), :],
                in0=eT[n][:].rearrange("p t n -> p n t"),
                in1=cg[h, u, c][:, :, blk(i)].rearrange("p t n -> p n t"),
                op=ALU.mult,
            )

        def v_ptq(h, u, c, a=0, b=512):
            codes, scales = ptq[h, u, c]
            nc.vector.quantize_mx(
                out=codes[:, a:b].bitcast(FP8X4), scales=scales[:, a:b], in_=pt[h, u, c][:, a:b, :].rearrange("p n t -> p (n t)")
            )

        def pe_pv(h, u, i, engine="s"):
            if i == 0:
                o[h, u] = outs.tile([P, 4, 512], F32, name="o", tag="o", bufs=2)
            po = psum.tile([P, 512], F32, name="po", tag="o", bufs=4)
            for c in range(2):
                mx(po[:], ptq[h, u, c], blk(i), vq[h, c], ALL, start=(c == 0), stop=(c == 1))
            copy_on(engine, o[h, u][:, i, :], po[:])

        def store_o(h, u, a, b):
            dst = out_0[h, 512 * u : 512 * u + 512, :].rearrange("(p t) n -> p t n", t=4)
            nc.sync.dma_start(out=dst[:, a:b, :], in_=o[h, u][:, a:b, :])

        def group_o(h, u, engine, a=0, b=512):
            if a == 0:
                ob[h, u] = stage.tile([P, 512, 4], BF16, name="ob", tag="grouped", bufs=4, align_bytes=64)
            copy_on(engine, ob[h, u][:, a:b, :], o[h, u][:, :, a:b].rearrange("p t n -> p n t"))

        def finish(h, u):
            wc = outs.tile([P, 512], U32, name="wc", tag="wc", bufs=2, align_bytes=64)
            ws = outs.tile([P, 512], U8, name="ws", tag="ws", bufs=2, align_bytes=64)
            nc.vector.quantize_mx(out=wc[:].bitcast(FP8X4), scales=ws[:], in_=ob[h, u][:].rearrange("p n t -> p (n t)"))
            cols = slice(512 * h, 512 * h + 512)
            nc.sync.dma_start(
                out=out_1[u, :, cols, :].rearrange("p m t -> p (m t)").bitcast(I32), in_=wc[:].bitcast(I32)
            )
            for Q in range(4):
                nc.sync.dma_start(
                    out=out_2[u, 4 * Q : 4 * Q + 4, cols].bitcast(I32), in_=ws[32 * Q : 32 * Q + 4, :].bitcast(I32)
                )

        raw["v", 0, 0] = load(v, 0, 0)
        raw["k", 1, 0] = load(k, 1, 0)
        raw["q", 1, 0] = load(q, 1, 0)
        raw["v", 0, 1] = load(v, 0, 1)
        raw["k", 1, 1] = load(k, 1, 1)
        raw["lm", 1] = load_lm(1)
        raw["q", 1, 1] = load(q, 1, 1)
        raw["v", 1, 0] = load(v, 1, 0)
        raw["v", 1, 1] = load(v, 1, 1)

        K00, Q00, K01, Q01 = ("k", 0, 0), ("q", 0, 0), ("k", 0, 1), ("q", 0, 1)
        K10, Q10, K11, Q11 = ("k", 1, 0), ("q", 1, 0), ("k", 1, 1), ("q", 1, 1)
        piece(K00, 0, "s")
        piece(K00, 1, "v")
        piece(Q00, 0, "s")
        quant(K00)
        piece(Q00, 1, "v")
        piece(K01, 0, "s")
        quant(Q00)
        piece(K01, 1, "s")
        nc.gpsimd.tensor_copy(out=gain_f[:], in_=gain_b[:])

        beside = {
            0: [(piece, Q01, 0), (piece, Q01, 1), (piece, ("lm", 0), 0), (v_group, 0, 0)],
            1: [(quant, Q01), (quant, ("lm", 0)), (pe_r, 0, 0), (v_group, 0, 1)],
            2: [(v_R, 0, 0), (piece, K10, 0), (piece, K10, 1)],
            3: [(v_nR, 0, 0), (s_L, 0, 0), (s_Z, 0, 0), (quant, ("v", 0, 0)), (piece, Q10, 0)],
            4: [(quant, K10), (pe_r, 0, 1), (piece, Q10, 1), (quant, ("v", 0, 1)), (v_group, 1, 0)],
            5: [(v_R, 0, 1), (quant, Q10), (piece, K11, 0), (piece, K11, 1)],
            6: [(v_nR, 0, 1), (s_L, 0, 1), (s_Z, 0, 1), (quant, ("v", 1, 0)), (quant, K11)],
            7: [(piece, ("lm", 1), 0), (piece, Q11, 0), (v_group, 1, 1)],
            8: [(quant, ("lm", 1)), (piece, Q11, 1), (s_ln, 0), (quant, ("v", 1, 1))],
            9: [(pe_lnz, 0, 0), (pe_lnz, 0, 1), (quant, Q11), (pe_r, 1, 0)],
            10: [(v_y, 0, 0), (v_R, 1, 0)],
            11: [(make_cg, 0, 0, 0), (v_nR, 1, 0), (v_y, 0, 1), (s_L, 1, 0), (s_Z, 1, 0)],
            12: [(make_cg, 0, 0, 1), (pe_r, 1, 1)],
            13: [(v_R, 1, 1), (make_cg, 0, 1, 0)],
            14: [(v_nR, 1, 1), (s_L, 1, 1), (s_Z, 1, 1)],
            15: [],
        }
        order = [(0, 0), (1, 0), (0, 1), (1, 1)] + [(i, c) for i in range(2, 16) for c in range(2)]
        LEAD = 2
        for j in range(LEAD):
            mm_s(*order[j])
        for j in range(len(order) + 1):
            if j + LEAD < len(order):
                if order[j + LEAD] == (0, 1):
                    quant(K01)
                mm_s(*order[j + LEAD])
            elif j + LEAD - len(order) < 3:
                pe_eT(j + LEAD - len(order))
            if j < len(order):
                vmax(*order[j])
            if j >= 1:
                i, c = order[j - 1]
                vsub(i, c)
                if c == 1:
                    s_exp(i)
                    if i >= 1:
                        pe_z(i - 1)
                    for f, *args in beside[i]:
                        f(*args)
        AHEAD = 3
        pe_eT(2) if 2 not in eT else None
        beside_c = {
            0: [(pe_z, 15), (s_ln, 1)],
            3: [(pe_lnz, 1, 0), (pe_lnz, 1, 1)],
            5: [(v_y, 1, 0)],
            6: [(v_y, 1, 1), (make_cg, 0, 1, 1)],
            7: [(make_cg, 1, 0, 0)],
            10: [(make_cg, 1, 0, 1)],
            14: [(make_cg, 1, 1, 0)],
            18: [(make_cg, 1, 1, 1)],
        }
        for n in range(32):
            if n + AHEAD < 32:
                pe_eT(n + AHEAD)
            v_tt(n)
            for f, *args in beside_c.get(n, []):
                f(*args)
            if n < 24:
                if n >= 4 and n % 4 == 0:
                    v_ptq(*steps[n - 1][:3])
            elif n == 24:
                v_ptq(*steps[23][:3])
            elif n == 28:
                v_ptq(1, 1, 0, 0, 256)
            elif n == 29:
                v_ptq(1, 1, 1, 0, 256)
            if n >= 8:
                h, u = steps[n - 8][:2]
                if n % 8 == 1:
                    pe_pv(h, u, 0)
                    pe_pv(h, u, 1)
                    store_o(h, u, 0, 2)
                if n % 8 == 3:
                    pe_pv(h, u, 2)
                    pe_pv(h, u, 3)
                    store_o(h, u, 2, 4)
                    group_o(h, u, "s")
            if n in (20, 28):
                finish(*steps[n - 16][:2])
            if n == 30:
                pe_pv(1, 1, 0)
                pe_pv(1, 1, 1)
                store_o(1, 1, 0, 2)
        v_ptq(1, 1, 0, 256, 512)
        v_ptq(1, 1, 1, 256, 512)
        finish(1, 0)
        pe_pv(1, 1, 2, "s")
        pe_pv(1, 1, 3, "v")
        store_o(1, 1, 2, 4)
        group_o(1, 1, "v", 0, 320)
        group_o(1, 1, "s", 320, 512)
        finish(1, 1)
